import numpy as np
import ml_dtypes


def mxq(x, axis, fmt="e4m3"):
    dtype, down = {"e4m3": (ml_dtypes.float8_e4m3fn, 7), "e5m2": (ml_dtypes.float8_e5m2, 14)}[fmt]
    v = np.moveaxis(np.asarray(x, np.float32).astype(ml_dtypes.bfloat16).astype(np.float64), axis, -1)
    blocks = v.reshape(v.shape[:-1] + (-1, 32))
    amax = np.abs(blocks).max(-1, keepdims=True)
    byte = np.maximum(np.where(amax > 0, np.frexp(amax)[1] - 1 + 127, 0) - down, 1)
    scale = np.exp2(byte - 127.0)
    codes = (blocks / scale).astype(np.float32).astype(dtype).astype(np.float64)
    return np.moveaxis((codes * scale).reshape(v.shape), -1, axis)


WIDE = False


def mx_kscale(k):
    if not WIDE:
        return np.ones(k)
    levels = np.array([10, -10, 5, -5, 0])
    if k % 512:
        return np.exp2(np.random.permutation(np.resize(levels, k // 32))).repeat(32)
    a = np.empty((k // 512, 16))
    for p in range(k // 512):
        a[p, :8] = np.random.permutation(np.resize(levels, 8))
        for g in range(8):
            far = levels[np.abs(levels - a[p, g]) >= 10]
            a[p, g + 8] = far[np.random.randint(len(far))]
    return np.exp2(a.ravel()).repeat(32)


def f64(x):
    return np.asarray(x).astype(np.float64)


def striped(idx):
    return np.tile(idx.reshape(-1, 16).T, (8, 1)).astype(np.uint16)


def unstriped(offs):
    return offs[:16].T.reshape(-1).astype(np.int64)


def pack_weight(w):
    k, n = w.shape
    w = f64(np.asarray(w, np.float32).astype(ml_dtypes.bfloat16)).reshape(k // 32, 32, n)
    amax = np.abs(w).max(1)
    byte = np.clip(np.where(amax > 0, np.frexp(amax)[1] - 1 + 127 - 7, 1), 1, 254)
    scaled = (w * np.exp2(127.0 - byte)[:, None, :]).reshape(k, n).astype(np.float32)
    words = np.ascontiguousarray(scaled.reshape(k // 512, 128, 4, n).transpose(0, 1, 3, 2)).astype(ml_dtypes.float8_e4m3fn).view(np.uint8)
    return words, np.ascontiguousarray(byte.astype(np.uint8).reshape(k // 512, 16, n))


def unpack_weight(words, scales):
    g, p, n, _ = words.shape
    vals = np.ascontiguousarray(words).view(ml_dtypes.float8_e4m3fn).astype(np.float64) * np.repeat(np.exp2(scales.astype(np.float64) - 127.0), 8, axis=1)[..., None]
    return vals.transpose(0, 1, 3, 2).reshape(g * 512, n)

def planes(y):
    n, m = y.shape
    v = y.astype(np.float32).astype(ml_dtypes.bfloat16).astype(np.float64).reshape(n // 32, 32, m)
    top = np.abs(v).max(1)
    byte = np.clip(np.where(top > 0, np.frexp(top)[1] - 1 + 127 - 7, 1), 1, 254)
    codes = (v * np.exp2(127.0 - byte)[:, None, :]).reshape(n, m).astype(np.float32).astype(ml_dtypes.float8_e4m3fn).view(np.uint8)
    words = codes.reshape(n // 512, 128, 4, m).transpose(0, 1, 3, 2)
    return np.ascontiguousarray(words), np.ascontiguousarray(byte.astype(np.uint8).reshape(n // 512, 16, m))


K, T, S, V, N = 512, 4096, 1024, 512, 512


def setup_inputs():
    n = np.random.standard_normal
    s = mx_kscale(K)[:, None]
    packed_xT = pack_weight(n((K, T)) * s)
    return {
        "x_words": packed_xT[0],
        "x_scales": packed_xT[1],
        "sT": (n((K, V)) * s).astype(np.float32),
        "w1": (n((K, N)) / np.sqrt(K) / s).astype(np.float32),
        "w2": (n((K, N)) / np.sqrt(K) / s).astype(np.float32),
        "offs": striped(np.random.permutation(T)[:S]),
        "par": striped(np.random.randint(0, V, S)),
    }


def reference(x_words, x_scales, sT, w1, w2, offs, par):
    xq = unpack_weight(x_words, x_scales)[:, unstriped(offs)]
    y = mxq(f64(w1), 0, "e4m3").T @ xq
    t = mxq(f64(w2), 0, "e4m3").T @ mxq(f64(sT), 0, "e4m3")
    out_0 = y + t[:, unstriped(par)]
    return (out_0,) + planes(out_0)

@@ -1,0 +1,188 @@
+from contextlib import ExitStack
+
+import concourse.mybir as mybir
+
+K, T, S, V, N = 512, 4096, 1024, 512, 512
+FLOPS = 2 * K * N * (S + V)
+
+F32 = mybir.dt.float32
+BF16 = mybir.dt.bfloat16
+I32 = mybir.dt.int32
+U32 = mybir.dt.uint32
+U16 = mybir.dt.uint16
+U8 = mybir.dt.uint8
+FP8X4 = mybir.dt.float8_e4m3fn_x4
+ADD = mybir.AluOpType.add
+
+P = 128
+PACK = 4
+HALF = 256
+BANK = 512
+PIECE = 256
+SPLIT = 128
+
+
+def tile_picked_fpn_none_po_kernel(tc, x_words, x_scales, sT, w1, w2, offs, par, out_0, out_1, out_2):
+    nc = tc.nc
+    with ExitStack() as ctx:
+        keep = ctx.enter_context(tc.tile_pool(name="keep", bufs=1))
+        psum = ctx.enter_context(tc.psum_pool(name="psum", bufs=1))
+
+        def tile(name, shape, dtype, tag=""):
+            return keep.tile(shape, dtype, name=name, tag=tag or name, align_bytes=64)
+
+        def load_columns(name, rows, h):
+            raw = tile(name, [P, PACK, HALF], F32)
+            nc.sync.dma_start(raw[:], rows.rearrange("(p j) c -> p j c", j=PACK)[:, :, h * HALF : (h + 1) * HALF])
+            return raw
+
+        warm = tile("warm", [P, 8], F32)
+        nc.gpsimd.memset(warm[:], 0.0)
+        nc.scalar.copy(warm[:, 1:2], warm[:, 0:1])
+        offs_sb = keep.tile([P, S // 16], U16, name="offs_sb")
+        par_sb = keep.tile([P, S // 16], U16, name="par_sb")
+        xs_all = tile("xs_all", [P, T], U8)
+        nc.vector.memset(xs_all[:].bitcast(I32), 0)
+        nc.scalar.dma_start(xs_all[:].bitcast(I32)[0:P:8, :], x_scales[0].bitcast(I32))
+        nc.sync.dma_start(offs_sb[:], offs)
+        w2_raw = [load_columns("w2_raw%d" % h, w2, h) for h in range(2)]
+        s_raw = [load_columns("s_raw%d" % h, sT, h) for h in range(2)]
+        nc.sync.dma_start(par_sb[:], par)
+        xw_all = tile("xw_all", [P, T], I32)
+        nc.sync.dma_start(xw_all[:], x_words[0].rearrange("p c r -> p (c r)").bitcast(I32))
+        w1_raw = [load_columns("w1_raw%d" % h, w1, h) for h in range(2)]
+
+        x_plane = tile("x_plane", [P, S], U8)
+        nc.vector.memset(x_plane[:].bitcast(I32), 0)
+        xs_kept = tile("xs_kept", [P, S], U8)
+        nc.vector.tensor_copy(xs_kept[:], xs_all[:].indirect(offs_sb[:]))
+
+        def deal(grouped, raw, h):
+            m = HALF // PACK
+            nc.scalar.copy(
+                grouped[:].rearrange("p t (m j) -> p m j t", j=PACK)[:, h * m : (h + 1) * m],
+                raw[:].rearrange("p j (m t) -> p m j t", t=PACK),
+            )
+
+        def weave(copy, grouped, rows, c0, c1):
+            copy(
+                grouped[:, PACK * c0 : PACK * c1].rearrange("p (c i t) -> p c t i", i=4, t=PACK),
+                rows[:, :, c0:c1].rearrange("p t (c i) -> p c t i", i=4),
+            )
+
+        def quantize(codes, plane, grouped):
+            nc.vector.quantize_mx(out=codes.bitcast(FP8X4), scales=plane, in_=grouped)
+
+        def product(bank, w_codes, w_plane, t, codes, plane):
+            nc.tensor.matmul_mx(
+                out=bank,
+                lhsT=w_codes[:, t * P : (t + 1) * P].bitcast(FP8X4),
+                lhsT_scale=w_plane[:, t * P : (t + 1) * P],
+                rhs=codes.bitcast(FP8X4),
+                rhs_scale=plane,
+                start=True,
+                stop=True,
+            )
+
+        w2_bf = tile("w2_bf", [P, PACK, N], BF16)
+        w2_codes = tile("w2_codes", [P, N], U32)
+        w2_plane = tile("w2_plane", [P, N], U8)
+        s_bf = [tile("s_bf%d" % h, [P, PACK * HALF], BF16) for h in range(2)]
+        s_codes = [tile("s_codes%d" % h, [P, HALF], U32) for h in range(2)]
+        s_plane = [tile("s_plane%d" % h, [P, HALF], U8) for h in range(2)]
+        for h in range(2):
+            deal(w2_bf, w2_raw[h], h)
+        weave(nc.vector.tensor_copy, s_bf[0], s_raw[0], 0, HALF)
+        quantize(w2_codes[:], w2_plane[:], w2_bf[:].rearrange("p t c -> p (t c)"))
+        quantize(s_codes[0][:], s_plane[0][:], s_bf[0][:])
+        weave(nc.scalar.copy, s_bf[1], s_raw[1], 0, SPLIT)
+        weave(nc.vector.tensor_copy, s_bf[1], s_raw[1], SPLIT, HALF)
+        quantize(s_codes[1][:], s_plane[1][:], s_bf[1][:])
+
+        coarse = [tile("coarse%d" % t, [P, V], F32) for t in range(PACK)]
+        banks = {}
+        for t in range(PACK):
+            for h in range(2):
+                banks[t, h] = psum.tile([P, BANK], F32, name="t_bank", tag="bank%d%d" % (t, h))
+                product(banks[t, h][:, :HALF], w2_codes, w2_plane, t, s_codes[h][:], s_plane[h][:])
+        for t in range(PACK):
+            for h in range(2):
+                nc.scalar.copy(coarse[t][:, h * HALF : (h + 1) * HALF], banks[t, h][:, :HALF])
+
+        for q in range(4):
+            nc.sync.dma_start(
+                x_plane[:].bitcast(I32)[32 * q : 32 * q + 4, :], xs_kept[:].bitcast(I32)[32 * q : 32 * q + 32 : 8, :]
+            )
+
+        def parents(c0, c1):
+            return par_sb[:, c0 // 16 : c1 // 16]
+
+        def fetch(name, c0, planes, tag=""):
+            got = tile(name, [P, len(planes), PIECE], F32, tag)
+            for i, t in enumerate(planes):
+                nc.vector.tensor_copy(got[:, i, :], coarse[t][:].indirect(parents(c0, c0 + PIECE)))
+            return [got[:, i, :] for i in range(len(planes))]
+
+        fetched = {0: fetch("fetched0", 0, range(PACK))}
+
+        x_codes = tile("x_codes", [P, S], U32)
+        nc.vector.tensor_copy(x_codes[:], xw_all[:].bitcast(U32).indirect(offs_sb[:]))
+        fetched[PIECE] = fetch("fetched1", PIECE, (0, 1), "xw_all")
+
+        w1_bf = tile("w1_bf", [P, PACK, N], BF16)
+        w1_codes = tile("w1_codes", [P, N], U32)
+        w1_plane = tile("w1_plane", [P, N], U8)
+        for h in range(2):
+            deal(w1_bf, w1_raw[h], h)
+        for t in range(PACK):
+            quantize(w1_codes[:, t * P : (t + 1) * P], w1_plane[:, t * P : (t + 1) * P], w1_bf[:, t, :])
+        fetched[PIECE] = fetched[PIECE] + fetch("fetched2", PIECE, (2, 3), "w1_bf")
+
+        for h in (1, 0):
+            cols = slice(h * BANK, (h + 1) * BANK)
+            for t in range(PACK):
+                banks[t, h] = psum.tile([P, BANK], F32, name="y_bank", tag="bank%d%d" % (t, h))
+                product(banks[t, h][:], w1_codes, w1_plane, t, x_codes[:, cols], x_plane[:, cols])
+
+        o_codes = tile("o_codes", [P, S], U32)
+        o_plane = tile("o_plane", [P, S], U8)
+        out_rows = out_0.rearrange("(p t) c -> p t c", t=PACK)
+        out_words = out_1[0].rearrange("p c r -> p (c r)").bitcast(I32)
+
+        def hand_out(result, c0, c1, copy):
+            n = c1 - c0
+            nc.sync.dma_start(out_rows[:, :, c0:c1], result[:])
+            grouped = tile("o_bf%d" % c0, [P, PACK * n], BF16)
+            weave(copy, grouped, result, 0, n)
+            a = 0
+            while a < n:
+                b = a + (256 if n - a >= 256 else 128)
+                quantize(o_codes[:, c0 + a : c0 + b], o_plane[:, c0 + a : c0 + b], grouped[:, PACK * a : PACK * b])
+                a = b
+            nc.sync.dma_start(out_words[:, c0:c1], o_codes[:].bitcast(I32)[:, c0:c1])
+
+        fine = [tile("fine%d" % t, [P, BANK], F32) for t in range(PACK)]
+        for t in range(PACK):
+            nc.scalar.copy(fine[t][:], banks[t, 1][:])
+
+        def add_parents(c0, c1, tag):
+            result = tile("result%d" % c0, [P, PACK, c1 - c0], F32, tag)
+            for t in range(PACK):
+                if c0 < BANK:
+                    nc.vector.tensor_tensor(result[:, t, :], banks[t, 0][:, c0:c1], fetched[c0][t], ADD)
+                else:
+                    nc.vector.tensor_tensor(
+                        result[:, t, :], coarse[t][:].indirect(parents(c0, c1)), fine[t][:, c0 - BANK : c1 - BANK], ADD
+                    )
+            return result
+
+        done = None
+        for c0, c1, tag in ((512, 768, ""), (0, 256, ""), (256, 512, ""), (768, 896, "xw_all"), (896, 1024, "w1_bf")):
+            result = add_parents(c0, c1, tag)
+            if done:
+                hand_out(*done, nc.scalar.copy)
+            done = (result, c0, c1)
+        hand_out(*done, nc.vector.tensor_copy)
+        for q in range(4):
+            queue = nc.scalar if q % 2 else nc.sync
+            queue.dma_start(out_2[0].bitcast(I32)[4 * q : 4 * q + 4, :], o_plane[:].bitcast(I32)[32 * q : 32 * q + 4, :])

@@ -18,8 +18,8 @@ P = 128
 PACK = 4
 HALF = 256
 BANK = 512
-PIECE = 256
-SPLIT = 128
+FIRST, EARLY, THIRD = 256, 640, 896
+S_SPLIT = 384
 
 
 def tile_picked_fpn_none_po_kernel(tc, x_words, x_scales, sT, w1, w2, offs, par, out_0, out_1, out_2):
@@ -31,10 +31,8 @@ def tile_picked_fpn_none_po_kernel(tc, x_words, x_scales, sT, w1, w2, offs, par,
         def tile(name, shape, dtype, tag=""):
             return keep.tile(shape, dtype, name=name, tag=tag or name, align_bytes=64)
 
-        def load_columns(name, rows, h):
-            raw = tile(name, [P, PACK, HALF], F32)
-            nc.sync.dma_start(raw[:], rows.rearrange("(p j) c -> p j c", j=PACK)[:, :, h * HALF : (h + 1) * HALF])
-            return raw
+        def by_partition(rows):
+            return rows.rearrange("(p j) c -> p j c", j=PACK)
 
         warm = tile("warm", [P, 8], F32)
         nc.gpsimd.memset(warm[:], 0.0)
@@ -43,26 +41,23 @@ def tile_picked_fpn_none_po_kernel(tc, x_words, x_scales, sT, w1, w2, offs, par,
         par_sb = keep.tile([P, S // 16], U16, name="par_sb")
         xs_all = tile("xs_all", [P, T], U8)
         nc.vector.memset(xs_all[:].bitcast(I32), 0)
-        nc.scalar.dma_start(xs_all[:].bitcast(I32)[0:P:8, :], x_scales[0].bitcast(I32))
         nc.sync.dma_start(offs_sb[:], offs)
-        w2_raw = [load_columns("w2_raw%d" % h, w2, h) for h in range(2)]
-        s_raw = [load_columns("s_raw%d" % h, sT, h) for h in range(2)]
+        s_raw = tile("s_raw", [P, PACK, V], F32)
+        w2_raw = tile("w2_raw", [P, PACK, N], F32)
+        w1_raw = tile("w1_raw", [P, PACK, N], F32)
+        nc.sync.dma_start(s_raw[:, :2, :], by_partition(sT)[:, :2, :])
+        nc.sync.dma_start(xs_all[:].bitcast(I32)[0:P:8, :], x_scales[0].bitcast(I32))
+        nc.sync.dma_start(s_raw[:, 2:, :], by_partition(sT)[:, 2:, :])
+        nc.sync.dma_start(w2_raw[:], by_partition(w2))
         nc.sync.dma_start(par_sb[:], par)
+        nc.sync.dma_start(w1_raw[:], by_partition(w1))
         xw_all = tile("xw_all", [P, T], I32)
         nc.sync.dma_start(xw_all[:], x_words[0].rearrange("p c r -> p (c r)").bitcast(I32))
-        w1_raw = [load_columns("w1_raw%d" % h, w1, h) for h in range(2)]
 
         x_plane = tile("x_plane", [P, S], U8)
         nc.vector.memset(x_plane[:].bitcast(I32), 0)
         xs_kept = tile("xs_kept", [P, S], U8)
         nc.vector.tensor_copy(xs_kept[:], xs_all[:].indirect(offs_sb[:]))
-
-        def deal(grouped, raw, h):
-            m = HALF // PACK
-            nc.scalar.copy(
-                grouped[:].rearrange("p t (m j) -> p m j t", j=PACK)[:, h * m : (h + 1) * m],
-                raw[:].rearrange("p j (m t) -> p m j t", t=PACK),
-            )
 
         def weave(copy, grouped, rows, c0, c1):
             copy(
@@ -84,30 +79,39 @@ def tile_picked_fpn_none_po_kernel(tc, x_words, x_scales, sT, w1, w2, offs, par,
                 stop=True,
             )
 
-        w2_bf = tile("w2_bf", [P, PACK, N], BF16)
         w2_codes = tile("w2_codes", [P, N], U32)
         w2_plane = tile("w2_plane", [P, N], U8)
-        s_bf = [tile("s_bf%d" % h, [P, PACK * HALF], BF16) for h in range(2)]
-        s_codes = [tile("s_codes%d" % h, [P, HALF], U32) for h in range(2)]
-        s_plane = [tile("s_plane%d" % h, [P, HALF], U8) for h in range(2)]
-        for h in range(2):
-            deal(w2_bf, w2_raw[h], h)
-        weave(nc.vector.tensor_copy, s_bf[0], s_raw[0], 0, HALF)
-        quantize(w2_codes[:], w2_plane[:], w2_bf[:].rearrange("p t c -> p (t c)"))
-        quantize(s_codes[0][:], s_plane[0][:], s_bf[0][:])
-        weave(nc.scalar.copy, s_bf[1], s_raw[1], 0, SPLIT)
-        weave(nc.vector.tensor_copy, s_bf[1], s_raw[1], SPLIT, HALF)
-        quantize(s_codes[1][:], s_plane[1][:], s_bf[1][:])
+        s_codes = tile("s_codes", [P, V], U32)
+        s_plane = tile("s_plane", [P, V], U8)
+        s_bf = tile("s_bf", [P, PACK * V], BF16)
+        weave(nc.scalar.copy, s_bf, s_raw, 0, HALF)
+        quantize(s_codes[:, :HALF], s_plane[:, :HALF], s_bf[:, : PACK * HALF])
+        weave(nc.scalar.copy, s_bf, s_raw, HALF, S_SPLIT)
+        weave(nc.vector.tensor_copy, s_bf, s_raw, S_SPLIT, V)
+        quantize(s_codes[:, HALF:], s_plane[:, HALF:], s_bf[:, PACK * HALF :])
+        def quantize_pair(name, raw, u, copy, codes, plane):
+            dealt = tile("%s_bf%d" % (name, u), [P, 2, N], BF16)
+            copy(
+                dealt[:].rearrange("p t (m j) -> p m j t", j=PACK),
+                raw[:].rearrange("p j (m t) -> p m j t", t=PACK)[:, :, :, 2 * u : 2 * u + 2],
+            )
+            for t in (2 * u, 2 * u + 1):
+                quantize(codes[:, t * P : (t + 1) * P], plane[:, t * P : (t + 1) * P], dealt[:, t - 2 * u, :])
+
+        quantize_pair("w2", w2_raw, 0, nc.vector.tensor_copy, w2_codes, w2_plane)
+        quantize_pair("w2", w2_raw, 1, nc.scalar.copy, w2_codes, w2_plane)
 
         coarse = [tile("coarse%d" % t, [P, V], F32) for t in range(PACK)]
-        banks = {}
-        for t in range(PACK):
-            for h in range(2):
-                banks[t, h] = psum.tile([P, BANK], F32, name="t_bank", tag="bank%d%d" % (t, h))
-                product(banks[t, h][:, :HALF], w2_codes, w2_plane, t, s_codes[h][:], s_plane[h][:])
-        for t in range(PACK):
-            for h in range(2):
-                nc.scalar.copy(coarse[t][:, h * HALF : (h + 1) * HALF], banks[t, h][:, :HALF])
+
+        def coarse_product(t, h, c0, c1, copy):
+            bank = psum.tile([P, BANK], F32, name="t_bank", tag="bank%d%d" % (t, h))
+            product(bank[:, : c1 - c0], w2_codes, w2_plane, t, s_codes[:, c0:c1], s_plane[:, c0:c1])
+            copy(coarse[t][:, c0:c1], bank[:, : c1 - c0])
+
+        coarse_product(0, 0, 0, HALF, nc.scalar.copy)
+        coarse_product(0, 1, HALF, V, nc.vector.tensor_copy)
+        for t in range(1, PACK):
+            coarse_product(t, 0, 0, V, nc.scalar.copy)
 
         for q in range(4):
             nc.sync.dma_start(
@@ -117,32 +121,38 @@ def tile_picked_fpn_none_po_kernel(tc, x_words, x_scales, sT, w1, w2, offs, par,
         def parents(c0, c1):
             return par_sb[:, c0 // 16 : c1 // 16]
 
-        def fetch(name, c0, planes, tag=""):
-            got = tile(name, [P, len(planes), PIECE], F32, tag)
-            for i, t in enumerate(planes):
-                nc.vector.tensor_copy(got[:, i, :], coarse[t][:].indirect(parents(c0, c0 + PIECE)))
-            return [got[:, i, :] for i in range(len(planes))]
+        fetched = tile("fetched", [P, PACK, EARLY - FIRST], F32)
+        for t in range(PACK):
+            nc.vector.tensor_copy(fetched[:, t, :], coarse[t][:].indirect(parents(FIRST, EARLY)))
 
-        fetched = {0: fetch("fetched0", 0, range(PACK))}
-
-        x_codes = tile("x_codes", [P, S], U32)
-        nc.vector.tensor_copy(x_codes[:], xw_all[:].bitcast(U32).indirect(offs_sb[:]))
-        fetched[PIECE] = fetch("fetched1", PIECE, (0, 1), "xw_all")
-
-        w1_bf = tile("w1_bf", [P, PACK, N], BF16)
         w1_codes = tile("w1_codes", [P, N], U32)
         w1_plane = tile("w1_plane", [P, N], U8)
+        x_codes = [tile("x_codes%d" % h, [P, BANK], U32) for h in range(2)]
         for h in range(2):
-            deal(w1_bf, w1_raw[h], h)
-        for t in range(PACK):
-            quantize(w1_codes[:, t * P : (t + 1) * P], w1_plane[:, t * P : (t + 1) * P], w1_bf[:, t, :])
-        fetched[PIECE] = fetched[PIECE] + fetch("fetched2", PIECE, (2, 3), "w1_bf")
+            quantize_pair("w1", w1_raw, h, nc.scalar.copy, w1_codes, w1_plane)
+            picks = offs_sb[:, h * BANK // 16 : (h + 1) * BANK // 16]
+            nc.vector.tensor_copy(x_codes[h][:], xw_all[:].bitcast(U32).indirect(picks))
 
-        for h in (1, 0):
-            cols = slice(h * BANK, (h + 1) * BANK)
+        def fine_products(c0, c1, h):
+            made = []
             for t in range(PACK):
-                banks[t, h] = psum.tile([P, BANK], F32, name="y_bank", tag="bank%d%d" % (t, h))
-                product(banks[t, h][:], w1_codes, w1_plane, t, x_codes[:, cols], x_plane[:, cols])
+                bank = psum.tile([P, BANK], F32, name="y_bank", tag="bank%d%d" % (t, h))
+                for a in range(c0, c1, 256):
+                    b = min(a + 256, c1)
+                    codes = x_codes[a // BANK][:, a % BANK : a % BANK + b - a]
+                    product(bank[:, a - c0 : b - c0], w1_codes, w1_plane, t, codes, x_plane[:, a:b])
+                made.append(bank[:, : c1 - c0])
+            return made
+
+        def to_sbuf(name, made, n):
+            fine = tile(name, [P, PACK, n], F32)
+            for t in range(PACK):
+                nc.scalar.copy(fine[:, t, :], made[t])
+            return fine
+
+        fine_first = to_sbuf("fine_first", fine_products(0, FIRST, 1), FIRST)
+        fine_early = fine_products(FIRST, EARLY, 0)
+        fine_late = to_sbuf("fine_late", fine_products(EARLY, S, 1), S - EARLY)
 
         o_codes = tile("o_codes", [P, S], U32)
         o_plane = tile("o_plane", [P, S], U8)
@@ -159,30 +169,31 @@ def tile_picked_fpn_none_po_kernel(tc, x_words, x_scales, sT, w1, w2, offs, par,
                 b = a + (256 if n - a >= 256 else 128)
                 quantize(o_codes[:, c0 + a : c0 + b], o_plane[:, c0 + a : c0 + b], grouped[:, PACK * a : PACK * b])
                 a = b
+
+        def store_words(c0, c1):
             nc.sync.dma_start(out_words[:, c0:c1], o_codes[:].bitcast(I32)[:, c0:c1])
 
-        fine = [tile("fine%d" % t, [P, BANK], F32) for t in range(PACK)]
-        for t in range(PACK):
-            nc.scalar.copy(fine[t][:], banks[t, 1][:])
-
-        def add_parents(c0, c1, tag):
+        def fetch_add(c0, c1, fine, at, tag=""):
             result = tile("result%d" % c0, [P, PACK, c1 - c0], F32, tag)
             for t in range(PACK):
-                if c0 < BANK:
-                    nc.vector.tensor_tensor(result[:, t, :], banks[t, 0][:, c0:c1], fetched[c0][t], ADD)
-                else:
-                    nc.vector.tensor_tensor(
-                        result[:, t, :], coarse[t][:].indirect(parents(c0, c1)), fine[t][:, c0 - BANK : c1 - BANK], ADD
-                    )
+                nc.vector.tensor_tensor(
+                    result[:, t, :], coarse[t][:].indirect(parents(c0, c1)), fine[:, t, c0 - at : c1 - at], ADD
+                )
             return result
 
-        done = None
-        for c0, c1, tag in ((512, 768, ""), (0, 256, ""), (256, 512, ""), (768, 896, "xw_all"), (896, 1024, "w1_bf")):
-            result = add_parents(c0, c1, tag)
-            if done:
-                hand_out(*done, nc.scalar.copy)
-            done = (result, c0, c1)
-        hand_out(*done, nc.vector.tensor_copy)
+        first = fetch_add(0, FIRST, fine_first, 0)
+        early = tile("early", [P, PACK, EARLY - FIRST], F32, "fine_first")
+        for t in range(PACK):
+            nc.vector.tensor_tensor(early[:, t, :], fine_early[t], fetched[:, t, :], ADD)
+        hand_out(first, 0, FIRST, nc.scalar.copy)
+        third = fetch_add(EARLY, THIRD, fine_late, EARLY, "fetched")
+        hand_out(early, FIRST, EARLY, nc.scalar.copy)
+        store_words(0, EARLY)
+        last = fetch_add(THIRD, S, fine_late, EARLY)
+        hand_out(third, EARLY, THIRD, nc.scalar.copy)
+        store_words(EARLY, THIRD)
+        hand_out(last, THIRD, S, nc.scalar.copy)
+        store_words(THIRD, S)
         for q in range(4):
             queue = nc.scalar if q % 2 else nc.sync
             queue.dma_start(out_2[0].bitcast(I32)[4 * q : 4 * q + 4, :], o_plane[:].bitcast(I32)[32 * q : 32 * q + 4, :])

from contextlib import ExitStack

import concourse.mybir as mybir

K, T, S, V, N = 512, 4096, 1024, 512, 512
FLOPS = 2 * K * N * (S + V)

F32 = mybir.dt.float32
BF16 = mybir.dt.bfloat16
I32 = mybir.dt.int32
U32 = mybir.dt.uint32
U16 = mybir.dt.uint16
U8 = mybir.dt.uint8
FP8X4 = mybir.dt.float8_e4m3fn_x4
ADD = mybir.AluOpType.add

P = 128
PACK = 4
HALF = 256
BANK = 512
FIRST, EARLY, THIRD = 256, 640, 896
S_SPLIT = 384


def tile_picked_fpn_none_po_kernel(tc, x_words, x_scales, sT, w1, w2, offs, par, out_0, out_1, out_2):
    nc = tc.nc
    with ExitStack() as ctx:
        keep = ctx.enter_context(tc.tile_pool(name="keep", bufs=1))
        psum = ctx.enter_context(tc.psum_pool(name="psum", bufs=1))

        def tile(name, shape, dtype, tag=""):
            return keep.tile(shape, dtype, name=name, tag=tag or name, align_bytes=64)

        def by_partition(rows):
            return rows.rearrange("(p j) c -> p j c", j=PACK)

        warm = tile("warm", [P, 8], F32)
        nc.gpsimd.memset(warm[:], 0.0)
        nc.scalar.copy(warm[:, 1:2], warm[:, 0:1])
        offs_sb = keep.tile([P, S // 16], U16, name="offs_sb")
        par_sb = keep.tile([P, S // 16], U16, name="par_sb")
        xs_all = tile("xs_all", [P, T], U8)
        nc.vector.memset(xs_all[:].bitcast(I32), 0)
        nc.sync.dma_start(offs_sb[:], offs)
        s_raw = tile("s_raw", [P, PACK, V], F32)
        w2_raw = tile("w2_raw", [P, PACK, N], F32)
        w1_raw = tile("w1_raw", [P, PACK, N], F32)
        nc.sync.dma_start(s_raw[:, :2, :], by_partition(sT)[:, :2, :])
        nc.sync.dma_start(xs_all[:].bitcast(I32)[0:P:8, :], x_scales[0].bitcast(I32))
        nc.sync.dma_start(s_raw[:, 2:, :], by_partition(sT)[:, 2:, :])
        nc.sync.dma_start(w2_raw[:], by_partition(w2))
        nc.sync.dma_start(par_sb[:], par)
        nc.sync.dma_start(w1_raw[:], by_partition(w1))
        xw_all = tile("xw_all", [P, T], I32)
        nc.sync.dma_start(xw_all[:], x_words[0].rearrange("p c r -> p (c r)").bitcast(I32))

        x_plane = tile("x_plane", [P, S], U8)
        nc.vector.memset(x_plane[:].bitcast(I32), 0)
        xs_kept = tile("xs_kept", [P, S], U8)
        nc.vector.tensor_copy(xs_kept[:], xs_all[:].indirect(offs_sb[:]))

        def weave(copy, grouped, rows, c0, c1):
            copy(
                grouped[:, PACK * c0 : PACK * c1].rearrange("p (c i t) -> p c t i", i=4, t=PACK),
                rows[:, :, c0:c1].rearrange("p t (c i) -> p c t i", i=4),
            )

        def quantize(codes, plane, grouped):
            nc.vector.quantize_mx(out=codes.bitcast(FP8X4), scales=plane, in_=grouped)

        def product(bank, w_codes, w_plane, t, codes, plane):
            nc.tensor.matmul_mx(
                out=bank,
                lhsT=w_codes[:, t * P : (t + 1) * P].bitcast(FP8X4),
                lhsT_scale=w_plane[:, t * P : (t + 1) * P],
                rhs=codes.bitcast(FP8X4),
                rhs_scale=plane,
                start=True,
                stop=True,
            )

        w2_codes = tile("w2_codes", [P, N], U32)
        w2_plane = tile("w2_plane", [P, N], U8)
        s_codes = tile("s_codes", [P, V], U32)
        s_plane = tile("s_plane", [P, V], U8)
        s_bf = tile("s_bf", [P, PACK * V], BF16)
        weave(nc.scalar.copy, s_bf, s_raw, 0, HALF)
        quantize(s_codes[:, :HALF], s_plane[:, :HALF], s_bf[:, : PACK * HALF])
        weave(nc.scalar.copy, s_bf, s_raw, HALF, S_SPLIT)
        weave(nc.vector.tensor_copy, s_bf, s_raw, S_SPLIT, V)
        quantize(s_codes[:, HALF:], s_plane[:, HALF:], s_bf[:, PACK * HALF :])
        def quantize_pair(name, raw, u, copy, codes, plane):
            dealt = tile("%s_bf%d" % (name, u), [P, 2, N], BF16)
            copy(
                dealt[:].rearrange("p t (m j) -> p m j t", j=PACK),
                raw[:].rearrange("p j (m t) -> p m j t", t=PACK)[:, :, :, 2 * u : 2 * u + 2],
            )
            for t in (2 * u, 2 * u + 1):
                quantize(codes[:, t * P : (t + 1) * P], plane[:, t * P : (t + 1) * P], dealt[:, t - 2 * u, :])

        quantize_pair("w2", w2_raw, 0, nc.vector.tensor_copy, w2_codes, w2_plane)
        quantize_pair("w2", w2_raw, 1, nc.scalar.copy, w2_codes, w2_plane)

        coarse = [tile("coarse%d" % t, [P, V], F32) for t in range(PACK)]

        def coarse_product(t, h, c0, c1, copy):
            bank = psum.tile([P, BANK], F32, name="t_bank", tag="bank%d%d" % (t, h))
            product(bank[:, : c1 - c0], w2_codes, w2_plane, t, s_codes[:, c0:c1], s_plane[:, c0:c1])
            copy(coarse[t][:, c0:c1], bank[:, : c1 - c0])

        coarse_product(0, 0, 0, HALF, nc.scalar.copy)
        coarse_product(0, 1, HALF, V, nc.vector.tensor_copy)
        for t in range(1, PACK):
            coarse_product(t, 0, 0, V, nc.scalar.copy)

        for q in range(4):
            nc.sync.dma_start(
                x_plane[:].bitcast(I32)[32 * q : 32 * q + 4, :], xs_kept[:].bitcast(I32)[32 * q : 32 * q + 32 : 8, :]
            )

        def parents(c0, c1):
            return par_sb[:, c0 // 16 : c1 // 16]

        fetched = tile("fetched", [P, PACK, EARLY - FIRST], F32)
        for t in range(PACK):
            nc.vector.tensor_copy(fetched[:, t, :], coarse[t][:].indirect(parents(FIRST, EARLY)))

        w1_codes = tile("w1_codes", [P, N], U32)
        w1_plane = tile("w1_plane", [P, N], U8)
        x_codes = [tile("x_codes%d" % h, [P, BANK], U32) for h in range(2)]
        for h in range(2):
            quantize_pair("w1", w1_raw, h, nc.scalar.copy, w1_codes, w1_plane)
            picks = offs_sb[:, h * BANK // 16 : (h + 1) * BANK // 16]
            nc.vector.tensor_copy(x_codes[h][:], xw_all[:].bitcast(U32).indirect(picks))

        def fine_products(c0, c1, h):
            made = []
            for t in range(PACK):
                bank = psum.tile([P, BANK], F32, name="y_bank", tag="bank%d%d" % (t, h))
                for a in range(c0, c1, 256):
                    b = min(a + 256, c1)
                    codes = x_codes[a // BANK][:, a % BANK : a % BANK + b - a]
                    product(bank[:, a - c0 : b - c0], w1_codes, w1_plane, t, codes, x_plane[:, a:b])
                made.append(bank[:, : c1 - c0])
            return made

        def to_sbuf(name, made, n):
            fine = tile(name, [P, PACK, n], F32)
            for t in range(PACK):
                nc.scalar.copy(fine[:, t, :], made[t])
            return fine

        fine_first = to_sbuf("fine_first", fine_products(0, FIRST, 1), FIRST)
        fine_early = fine_products(FIRST, EARLY, 0)
        fine_late = to_sbuf("fine_late", fine_products(EARLY, S, 1), S - EARLY)

        o_codes = tile("o_codes", [P, S], U32)
        o_plane = tile("o_plane", [P, S], U8)
        out_rows = out_0.rearrange("(p t) c -> p t c", t=PACK)
        out_words = out_1[0].rearrange("p c r -> p (c r)").bitcast(I32)

        def hand_out(result, c0, c1, copy):
            n = c1 - c0
            nc.sync.dma_start(out_rows[:, :, c0:c1], result[:])
            grouped = tile("o_bf%d" % c0, [P, PACK * n], BF16)
            weave(copy, grouped, result, 0, n)
            a = 0
            while a < n:
                b = a + (256 if n - a >= 256 else 128)
                quantize(o_codes[:, c0 + a : c0 + b], o_plane[:, c0 + a : c0 + b], grouped[:, PACK * a : PACK * b])
                a = b

        def store_words(c0, c1):
            nc.sync.dma_start(out_words[:, c0:c1], o_codes[:].bitcast(I32)[:, c0:c1])

        def fetch_add(c0, c1, fine, at, tag=""):
            result = tile("result%d" % c0, [P, PACK, c1 - c0], F32, tag)
            for t in range(PACK):
                nc.vector.tensor_tensor(
                    result[:, t, :], coarse[t][:].indirect(parents(c0, c1)), fine[:, t, c0 - at : c1 - at], ADD
                )
            return result

        first = fetch_add(0, FIRST, fine_first, 0)
        early = tile("early", [P, PACK, EARLY - FIRST], F32, "fine_first")
        for t in range(PACK):
            nc.vector.tensor_tensor(early[:, t, :], fine_early[t], fetched[:, t, :], ADD)
        hand_out(first, 0, FIRST, nc.scalar.copy)
        third = fetch_add(EARLY, THIRD, fine_late, EARLY, "fetched")
        hand_out(early, FIRST, EARLY, nc.scalar.copy)
        store_words(0, EARLY)
        last = fetch_add(THIRD, S, fine_late, EARLY)
        hand_out(third, EARLY, THIRD, nc.scalar.copy)
        store_words(EARLY, THIRD)
        hand_out(last, THIRD, S, nc.scalar.copy)
        store_words(THIRD, S)
        for q in range(4):
            queue = nc.scalar if q % 2 else nc.sync
            queue.dma_start(out_2[0].bitcast(I32)[4 * q : 4 * q + 4, :], o_plane[:].bitcast(I32)[32 * q : 32 * q + 4, :])
